import numpy as np
CORES = [16,17,18,19,20,21,22,23,184,185,186,187,188,189,190,191]
N = 16
ROUNDS = 4
def setup_inputs(rng):
    return {"x": rng.standard_normal((N, ROUNDS, 128, 256), dtype=np.float32)}
def reference(x):
    b = 256 // N
    blocks = x.reshape(N, ROUNDS, 128, N, b)
    return {"y": np.ascontiguousarray(blocks.transpose(3, 1, 2, 0, 4)).reshape(N, ROUNDS, 128, 256)}

@@ -1,0 +1,152 @@
+import concourse.bass as bass
+
+ROUNDS = 4
+N = 16
+B = 256 // N
+HALF = 128
+GATEWAYS = (2, 3, 6, 7)
+
+SCRATCH = {
+    "z": ("sbuf", [128, 768], "float32"),
+}
+SEMAPHORES = ["loc", "sent", "arr0", "arr1", "aux0", "aux1"]
+
+
+def is_gateway(rank):
+    return rank % 8 in GATEWAYS
+
+
+def send_base(rank, k):
+    return 256 * (k % 2) if is_gateway(rank) else 256 * ((k + 1) % 3)
+
+
+def land_base(rank, k):
+    return 256 * ((k + 1) % 2) if is_gateway(rank) else 256 * (k % 3)
+
+
+def pass_base(k):
+    return 512 + HALF * (k % 2)
+
+
+def rank_program(g, core, T, topo):
+    me = T.rank_of(core)
+    if me is None:
+        return
+    z = T.z
+    sem = T.sem
+    aux = (sem.aux0, sem.aux1)
+    chip = me // 8
+    near = [r for r in range(8 * chip, 8 * chip + 8) if r != me]
+    far = list(range(8 * (1 - chip), 8 * (1 - chip) + 8))
+    count = {"loc": 0, "sent": 0}
+
+    def arrival_sem(rank, k):
+        if is_gateway(rank):
+            return (sem.arr0, sem.arr1)[k % 2]
+        return (sem.arr0, sem.arr1, sem.aux0, sem.aux1)[k]
+
+    def local(out, in_):
+        g.dma_start(out, in_).then_inc(sem.loc, 16)
+        count["loc"] += 16
+
+    def wait_local():
+        g.wait_ge(sem.loc, count["loc"])
+
+    def wait_sent():
+        g.wait_ge(sem.sent, count["sent"])
+
+    def load(k):
+        s = send_base(me, k)
+        local(z[:, s:s + 256], T.x[k])
+
+    def store(k):
+        s = land_base(me, k)
+        local(T.y[k], z[:, s:s + 256])
+
+    def wait_round(k):
+        g.wait_ge(arrival_sem(me, k), 15 * (k // 2 + 1) if is_gateway(me) else 15)
+
+    def block(k, src_col, origin, dst, engine):
+        rid, pid = topo.addr(T.cores[dst], core)
+        d = land_base(dst, k) + B * origin
+        return bass.RemoteDMATransfer(dst_ids=[bass.DstId(rid=rid, pnc=pid)], dma_engine_mask=1 << engine,
+                                      remote_sem=arrival_sem(dst, k), src=z[:, src_col:src_col + B], dst=z[:, d:d + B])
+
+    def fused(transfers):
+        g.remote_dma_fused(transfers, local_sem=sem.sent)
+        count["sent"] += len(transfers)
+
+    def own(k, dsts, first_engine):
+        s = send_base(me, k)
+        return [block(k, s + B * d, me, d, first_engine + i) for i, d in enumerate(dsts)]
+
+    def own_block_of_round_0():
+        d = land_base(me, 0) + B * me
+        local(z[:, d:d + B], T.x[0, :, B * me:B * (me + 1)])
+
+    def finish():
+        wait_local()
+        local(T.y[1:ROUNDS, :, B * me:B * (me + 1)], T.x[1:ROUNDS, :, B * me:B * (me + 1)])
+        wait_local()
+        wait_sent()
+
+    if not is_gateway(me):
+        gate = me + 2
+        rid, pid = topo.addr(T.cores[gate], core)
+
+        def hand_over(k):
+            s = send_base(me, k) + HALF * (1 - chip)
+            f = pass_base(k)
+            g.remote_dma(z[:, f:f + HALF], z[:, s:s + HALF], aux[k % 2], sem.sent, pid, rid, 0xFFFF)
+            count["sent"] += 16
+
+        load(0)
+        load(1)
+        own_block_of_round_0()
+        wait_local()
+        hand_over(0)
+        hand_over(1)
+        fused(own(0, near, 0))
+        for k in range(1, ROUNDS):
+            wait_round(k - 1)
+            fused(own(k, near, 0))
+            store(k - 1)
+            if k + 1 < ROUNDS:
+                wait_local()
+                load(k + 1)
+                wait_local()
+                hand_over(k + 1)
+        wait_round(ROUNDS - 1)
+        store(ROUNDS - 1)
+        finish()
+        return
+
+    mate = me - 2
+    far_partners = [d for d in far if not is_gateway(d)]
+    far_gateways = [d for d in far if is_gateway(d)]
+
+    def passed(k, dsts, first_engine):
+        f = pass_base(k)
+        return [block(k, f + B * (d % 8), mate, d, first_engine + i) for i, d in enumerate(dsts)]
+
+    own_block_of_round_0()
+    for k in range(ROUNDS):
+        if k > 0:
+            wait_round(k - 1)
+            store(k - 1)
+            wait_local()
+        load(k)
+        wait_local()
+        g.wait_ge(aux[k % 2], 16 * (k // 2 + 1))
+        frees_f = k + 2 < ROUNDS
+        first_near = [d for d in near if d != mate] if frees_f else near
+        fused(own(k, far_partners, 0) + passed(k, far_partners, 4) + own(k, first_near, 8))
+        if k + 1 < ROUNDS:
+            wait_sent()
+        fused(own(k, far_gateways, 0) + passed(k, far_gateways, 4))
+        if frees_f:
+            wait_sent()
+            fused(own(k, [mate], 8))
+    wait_round(ROUNDS - 1)
+    store(ROUNDS - 1)
+    finish()

@@ -5,11 +5,14 @@ N = 16
 B = 256 // N
 HALF = 128
 GATEWAYS = (2, 3, 6, 7)
+OWN_LEVEL = (1, 3, 4, 6)
+PASS_LEVEL = (2, 3, 5, 6)
+HAND_LEVEL = (1, 1, 4, 5)
 
 SCRATCH = {
     "z": ("sbuf", [128, 768], "float32"),
 }
-SEMAPHORES = ["loc", "sent", "arr0", "arr1", "aux0", "aux1"]
+SEMAPHORES = ["loc", "sent", "lvl0", "lvl1", "lvl2", "lvl3"]
 
 
 def is_gateway(rank):
@@ -34,16 +37,11 @@ def rank_program(g, core, T, topo):
         return
     z = T.z
     sem = T.sem
-    aux = (sem.aux0, sem.aux1)
+    lvl = (sem.lvl0, sem.lvl1, sem.lvl2, sem.lvl3)
     chip = me // 8
     near = [r for r in range(8 * chip, 8 * chip + 8) if r != me]
     far = list(range(8 * (1 - chip), 8 * (1 - chip) + 8))
-    count = {"loc": 0, "sent": 0}
-
-    def arrival_sem(rank, k):
-        if is_gateway(rank):
-            return (sem.arr0, sem.arr1)[k % 2]
-        return (sem.arr0, sem.arr1, sem.aux0, sem.aux1)[k]
+    count = {"loc": 0, "sent": 0, 0: 0, 1: 0, 2: 0, 3: 0}
 
     def local(out, in_):
         g.dma_start(out, in_).then_inc(sem.loc, 16)
@@ -55,6 +53,11 @@ def rank_program(g, core, T, topo):
     def wait_sent():
         g.wait_ge(sem.sent, count["sent"])
 
+    def wait_level(level, adds):
+        i = (level - 1) % 4
+        count[i] += adds
+        g.wait_ge(lvl[i], count[i])
+
     def load(k):
         s = send_base(me, k)
         local(z[:, s:s + 256], T.x[k])
@@ -63,90 +66,100 @@ def rank_program(g, core, T, topo):
         s = land_base(me, k)
         local(T.y[k], z[:, s:s + 256])
 
-    def wait_round(k):
-        g.wait_ge(arrival_sem(me, k), 15 * (k // 2 + 1) if is_gateway(me) else 15)
+    def store_and_load(k_store, k_load):
+        store(k_store)
+        wait_local()
+        load(k_load)
+        wait_local()
 
-    def block(k, src_col, origin, dst, engine):
+    def transfer(dst, level, mask, src, out):
         rid, pid = topo.addr(T.cores[dst], core)
-        d = land_base(dst, k) + B * origin
-        return bass.RemoteDMATransfer(dst_ids=[bass.DstId(rid=rid, pnc=pid)], dma_engine_mask=1 << engine,
-                                      remote_sem=arrival_sem(dst, k), src=z[:, src_col:src_col + B], dst=z[:, d:d + B])
+        return bass.RemoteDMATransfer(dst_ids=[bass.DstId(rid=rid, pnc=pid)], dma_engine_mask=mask,
+                                      remote_sem=lvl[(level - 1) % 4], src=src, dst=out)
 
-    def fused(transfers):
+    def block(k, level, src_col, origin, dst, engine):
+        d = land_base(dst, k) + B * origin
+        return transfer(dst, level, 1 << engine, z[:, src_col:src_col + B], z[:, d:d + B])
+
+    def fused(transfers, engines_each=1):
         g.remote_dma_fused(transfers, local_sem=sem.sent)
-        count["sent"] += len(transfers)
+        count["sent"] += engines_each * len(transfers)
 
     def own(k, dsts, first_engine):
         s = send_base(me, k)
-        return [block(k, s + B * d, me, d, first_engine + i) for i, d in enumerate(dsts)]
+        return [block(k, OWN_LEVEL[k], s + B * d, me, d, first_engine + i) for i, d in enumerate(dsts)]
 
     def own_block_of_round_0():
         d = land_base(me, 0) + B * me
         local(z[:, d:d + B], T.x[0, :, B * me:B * (me + 1)])
 
     def finish():
+        store(ROUNDS - 1)
         wait_local()
         local(T.y[1:ROUNDS, :, B * me:B * (me + 1)], T.x[1:ROUNDS, :, B * me:B * (me + 1)])
         wait_local()
         wait_sent()
 
     if not is_gateway(me):
-        gate = me + 2
-        rid, pid = topo.addr(T.cores[gate], core)
-
-        def hand_over(k):
+        def hand(k, mask):
             s = send_base(me, k) + HALF * (1 - chip)
             f = pass_base(k)
-            g.remote_dma(z[:, f:f + HALF], z[:, s:s + HALF], aux[k % 2], sem.sent, pid, rid, 0xFFFF)
-            count["sent"] += 16
+            return transfer(me + 2, HAND_LEVEL[k], mask, z[:, s:s + HALF], z[:, f:f + HALF])
 
         load(0)
         load(1)
         own_block_of_round_0()
         wait_local()
-        hand_over(0)
-        hand_over(1)
+        fused([hand(0, 0x00FF), hand(1, 0xFF00)], 8)
         fused(own(0, near, 0))
-        for k in range(1, ROUNDS):
-            wait_round(k - 1)
-            fused(own(k, near, 0))
-            store(k - 1)
-            if k + 1 < ROUNDS:
-                wait_local()
-                load(k + 1)
-                wait_local()
-                hand_over(k + 1)
-        wait_round(ROUNDS - 1)
-        store(ROUNDS - 1)
+        wait_level(1, 11)
+        wait_level(2, 4)
+        fused(own(1, near, 0))
+        store_and_load(0, 2)
+        wait_level(3, 15)
+        fused(own(2, near, 0))
+        fused([hand(2, 0xFFFF)], 16)
+        store_and_load(1, 3)
+        wait_level(4, 11)
+        fused([hand(3, 0xFFFF)], 16)
+        wait_level(5, 4)
+        fused(own(3, near, 0))
+        store(2)
+        wait_level(6, 15)
         finish()
         return
 
     mate = me - 2
-    far_partners = [d for d in far if not is_gateway(d)]
-    far_gateways = [d for d in far if is_gateway(d)]
 
-    def passed(k, dsts, first_engine):
+    def passed(k):
         f = pass_base(k)
-        return [block(k, f + B * (d % 8), mate, d, first_engine + i) for i, d in enumerate(dsts)]
+        return [block(k, PASS_LEVEL[k], f + B * (d % 8), mate, d, i) for i, d in enumerate(far)]
+
+    def own_all(k):
+        return own(k, far, 0) + own(k, near, 8)
 
     own_block_of_round_0()
-    for k in range(ROUNDS):
-        if k > 0:
-            wait_round(k - 1)
-            store(k - 1)
-            wait_local()
-        load(k)
-        wait_local()
-        g.wait_ge(aux[k % 2], 16 * (k // 2 + 1))
-        frees_f = k + 2 < ROUNDS
-        first_near = [d for d in near if d != mate] if frees_f else near
-        fused(own(k, far_partners, 0) + passed(k, far_partners, 4) + own(k, first_near, 8))
-        if k + 1 < ROUNDS:
-            wait_sent()
-        fused(own(k, far_gateways, 0) + passed(k, far_gateways, 4))
-        if frees_f:
-            wait_sent()
-            fused(own(k, [mate], 8))
-    wait_round(ROUNDS - 1)
-    store(ROUNDS - 1)
+    load(0)
+    wait_local()
+    fused(own_all(0))
+    wait_level(1, 11 + 8 + 8)
+    wait_sent()
+    fused(passed(0))
+    wait_level(2, 4)
+    store_and_load(0, 1)
+    wait_sent()
+    fused(own_all(1))
+    fused(passed(1))
+    wait_level(3, 15)
+    store_and_load(1, 2)
+    wait_sent()
+    fused(own_all(2))
+    wait_level(4, 11 + 16)
+    wait_sent()
+    fused(passed(2))
+    wait_level(5, 4 + 16)
+    store_and_load(2, 3)
+    fused(own_all(3))
+    fused(passed(3))
+    wait_level(6, 15)
     finish()

@@ -5,14 +5,15 @@ N = 16
 B = 256 // N
 HALF = 128
 GATEWAYS = (2, 3, 6, 7)
-OWN_LEVEL = (1, 3, 4, 6)
-PASS_LEVEL = (2, 3, 5, 6)
-HAND_LEVEL = (1, 1, 4, 5)
+OWN_AT_PARTNER = (0, 2, 3, 1)
+PASS_AT_PARTNER = (1, 2, 0, 1)
+BLOCK_AT_GATEWAY = (1, 2, 3, 1)
+HAND_AT_GATEWAY = (0, 1, 0, 3)
 
 SCRATCH = {
     "z": ("sbuf", [128, 768], "float32"),
 }
-SEMAPHORES = ["loc", "sent", "lvl0", "lvl1", "lvl2", "lvl3"]
+SEMAPHORES = ["loc", "sent", "c0", "c1", "c2", "c3"]
 
 
 def is_gateway(rank):
@@ -37,7 +38,7 @@ def rank_program(g, core, T, topo):
         return
     z = T.z
     sem = T.sem
-    lvl = (sem.lvl0, sem.lvl1, sem.lvl2, sem.lvl3)
+    c = (sem.c0, sem.c1, sem.c2, sem.c3)
     chip = me // 8
     near = [r for r in range(8 * chip, 8 * chip + 8) if r != me]
     far = list(range(8 * (1 - chip), 8 * (1 - chip) + 8))
@@ -53,10 +54,9 @@ def rank_program(g, core, T, topo):
     def wait_sent():
         g.wait_ge(sem.sent, count["sent"])
 
-    def wait_level(level, adds):
-        i = (level - 1) % 4
+    def wait_more(i, adds):
         count[i] += adds
-        g.wait_ge(lvl[i], count[i])
+        g.wait_ge(c[i], count[i])
 
     def load(k):
         s = send_base(me, k)
@@ -72,14 +72,15 @@ def rank_program(g, core, T, topo):
         load(k_load)
         wait_local()
 
-    def transfer(dst, level, mask, src, out):
+    def transfer(dst, i, mask, src, out):
         rid, pid = topo.addr(T.cores[dst], core)
         return bass.RemoteDMATransfer(dst_ids=[bass.DstId(rid=rid, pnc=pid)], dma_engine_mask=mask,
-                                      remote_sem=lvl[(level - 1) % 4], src=src, dst=out)
+                                      remote_sem=c[i], src=src, dst=out)
 
-    def block(k, level, src_col, origin, dst, engine):
+    def block(k, at_partner, src_col, origin, dst, engine):
         d = land_base(dst, k) + B * origin
-        return transfer(dst, level, 1 << engine, z[:, src_col:src_col + B], z[:, d:d + B])
+        i = BLOCK_AT_GATEWAY[k] if is_gateway(dst) else at_partner[k]
+        return transfer(dst, i, 1 << engine, z[:, src_col:src_col + B], z[:, d:d + B])
 
     def fused(transfers, engines_each=1):
         g.remote_dma_fused(transfers, local_sem=sem.sent)
@@ -87,7 +88,7 @@ def rank_program(g, core, T, topo):
 
     def own(k, dsts, first_engine):
         s = send_base(me, k)
-        return [block(k, OWN_LEVEL[k], s + B * d, me, d, first_engine + i) for i, d in enumerate(dsts)]
+        return [block(k, OWN_AT_PARTNER, s + B * d, me, d, first_engine + i) for i, d in enumerate(dsts)]
 
     def own_block_of_round_0():
         d = land_base(me, 0) + B * me
@@ -101,31 +102,32 @@ def rank_program(g, core, T, topo):
         wait_sent()
 
     if not is_gateway(me):
-        def hand(k, mask):
+        def hand(k):
             s = send_base(me, k) + HALF * (1 - chip)
             f = pass_base(k)
-            return transfer(me + 2, HAND_LEVEL[k], mask, z[:, s:s + HALF], z[:, f:f + HALF])
+            fused([transfer(me + 2, HAND_AT_GATEWAY[k], 0xFFFF, z[:, s:s + HALF], z[:, f:f + HALF])], 16)
 
         load(0)
         load(1)
         own_block_of_round_0()
         wait_local()
-        fused([hand(0, 0x00FF), hand(1, 0xFF00)], 8)
+        hand(0)
         fused(own(0, near, 0))
-        wait_level(1, 11)
-        wait_level(2, 4)
+        wait_more(0, 11)
+        hand(1)
+        wait_more(1, 4)
         fused(own(1, near, 0))
         store_and_load(0, 2)
-        wait_level(3, 15)
+        wait_more(2, 15)
         fused(own(2, near, 0))
-        fused([hand(2, 0xFFFF)], 16)
+        hand(2)
         store_and_load(1, 3)
-        wait_level(4, 11)
-        fused([hand(3, 0xFFFF)], 16)
-        wait_level(5, 4)
+        wait_more(3, 11)
+        hand(3)
+        wait_more(0, 4)
         fused(own(3, near, 0))
         store(2)
-        wait_level(6, 15)
+        wait_more(1, 15)
         finish()
         return
 
@@ -133,7 +135,7 @@ def rank_program(g, core, T, topo):
 
     def passed(k):
         f = pass_base(k)
-        return [block(k, PASS_LEVEL[k], f + B * (d % 8), mate, d, i) for i, d in enumerate(far)]
+        return [block(k, PASS_AT_PARTNER, f + B * (d % 8), mate, d, i) for i, d in enumerate(far)]
 
     def own_all(k):
         return own(k, far, 0) + own(k, near, 8)
@@ -142,24 +144,22 @@ def rank_program(g, core, T, topo):
     load(0)
     wait_local()
     fused(own_all(0))
-    wait_level(1, 11 + 8 + 8)
-    wait_sent()
+    wait_more(0, 16)
     fused(passed(0))
-    wait_level(2, 4)
+    wait_more(1, 15 + 16)
     store_and_load(0, 1)
     wait_sent()
     fused(own_all(1))
     fused(passed(1))
-    wait_level(3, 15)
+    wait_more(2, 15)
     store_and_load(1, 2)
     wait_sent()
     fused(own_all(2))
-    wait_level(4, 11 + 16)
-    wait_sent()
+    wait_more(0, 16)
     fused(passed(2))
-    wait_level(5, 4 + 16)
+    wait_more(3, 15 + 16)
     store_and_load(2, 3)
     fused(own_all(3))
     fused(passed(3))
-    wait_level(6, 15)
+    wait_more(1, 15)
     finish()

@@ -8,7 +8,7 @@ GATEWAYS = (2, 3, 6, 7)
 OWN_AT_PARTNER = (0, 2, 3, 1)
 PASS_AT_PARTNER = (1, 2, 0, 1)
 BLOCK_AT_GATEWAY = (1, 2, 3, 1)
-HAND_AT_GATEWAY = (0, 1, 0, 3)
+HAND_AT_GATEWAY = (0, 1, 0, 2)
 
 SCRATCH = {
     "z": ("sbuf", [128, 768], "float32"),
@@ -157,9 +157,10 @@ def rank_program(g, core, T, topo):
     fused(own_all(2))
     wait_more(0, 16)
     fused(passed(2))
-    wait_more(3, 15 + 16)
+    wait_more(3, 15)
     store_and_load(2, 3)
     fused(own_all(3))
+    wait_more(2, 16)
     fused(passed(3))
     wait_more(1, 15)
     finish()

import concourse.bass as bass

ROUNDS = 4
N = 16
B = 256 // N
HALF = 128
GATEWAYS = (2, 3, 6, 7)
OWN_AT_PARTNER = (0, 2, 3, 1)
PASS_AT_PARTNER = (1, 2, 0, 1)
BLOCK_AT_GATEWAY = (1, 2, 3, 1)
HAND_AT_GATEWAY = (0, 1, 0, 2)

SCRATCH = {
    "z": ("sbuf", [128, 768], "float32"),
}
SEMAPHORES = ["loc", "sent", "c0", "c1", "c2", "c3"]


def is_gateway(rank):
    return rank % 8 in GATEWAYS


def send_base(rank, k):
    return 256 * (k % 2) if is_gateway(rank) else 256 * ((k + 1) % 3)


def land_base(rank, k):
    return 256 * ((k + 1) % 2) if is_gateway(rank) else 256 * (k % 3)


def pass_base(k):
    return 512 + HALF * (k % 2)


def rank_program(g, core, T, topo):
    me = T.rank_of(core)
    if me is None:
        return
    z = T.z
    sem = T.sem
    c = (sem.c0, sem.c1, sem.c2, sem.c3)
    chip = me // 8
    near = [r for r in range(8 * chip, 8 * chip + 8) if r != me]
    far = list(range(8 * (1 - chip), 8 * (1 - chip) + 8))
    count = {"loc": 0, "sent": 0, 0: 0, 1: 0, 2: 0, 3: 0}

    def local(out, in_):
        g.dma_start(out, in_).then_inc(sem.loc, 16)
        count["loc"] += 16

    def wait_local():
        g.wait_ge(sem.loc, count["loc"])

    def wait_sent():
        g.wait_ge(sem.sent, count["sent"])

    def wait_more(i, adds):
        count[i] += adds
        g.wait_ge(c[i], count[i])

    def load(k):
        s = send_base(me, k)
        local(z[:, s:s + 256], T.x[k])

    def store(k):
        s = land_base(me, k)
        local(T.y[k], z[:, s:s + 256])

    def store_and_load(k_store, k_load):
        store(k_store)
        wait_local()
        load(k_load)
        wait_local()

    def transfer(dst, i, mask, src, out):
        rid, pid = topo.addr(T.cores[dst], core)
        return bass.RemoteDMATransfer(dst_ids=[bass.DstId(rid=rid, pnc=pid)], dma_engine_mask=mask,
                                      remote_sem=c[i], src=src, dst=out)

    def block(k, at_partner, src_col, origin, dst, engine):
        d = land_base(dst, k) + B * origin
        i = BLOCK_AT_GATEWAY[k] if is_gateway(dst) else at_partner[k]
        return transfer(dst, i, 1 << engine, z[:, src_col:src_col + B], z[:, d:d + B])

    def fused(transfers, engines_each=1):
        g.remote_dma_fused(transfers, local_sem=sem.sent)
        count["sent"] += engines_each * len(transfers)

    def own(k, dsts, first_engine):
        s = send_base(me, k)
        return [block(k, OWN_AT_PARTNER, s + B * d, me, d, first_engine + i) for i, d in enumerate(dsts)]

    def own_block_of_round_0():
        d = land_base(me, 0) + B * me
        local(z[:, d:d + B], T.x[0, :, B * me:B * (me + 1)])

    def finish():
        store(ROUNDS - 1)
        wait_local()
        local(T.y[1:ROUNDS, :, B * me:B * (me + 1)], T.x[1:ROUNDS, :, B * me:B * (me + 1)])
        wait_local()
        wait_sent()

    if not is_gateway(me):
        def hand(k):
            s = send_base(me, k) + HALF * (1 - chip)
            f = pass_base(k)
            fused([transfer(me + 2, HAND_AT_GATEWAY[k], 0xFFFF, z[:, s:s + HALF], z[:, f:f + HALF])], 16)

        load(0)
        load(1)
        own_block_of_round_0()
        wait_local()
        hand(0)
        fused(own(0, near, 0))
        wait_more(0, 11)
        hand(1)
        wait_more(1, 4)
        fused(own(1, near, 0))
        store_and_load(0, 2)
        wait_more(2, 15)
        fused(own(2, near, 0))
        hand(2)
        store_and_load(1, 3)
        wait_more(3, 11)
        hand(3)
        wait_more(0, 4)
        fused(own(3, near, 0))
        store(2)
        wait_more(1, 15)
        finish()
        return

    mate = me - 2

    def passed(k):
        f = pass_base(k)
        return [block(k, PASS_AT_PARTNER, f + B * (d % 8), mate, d, i) for i, d in enumerate(far)]

    def own_all(k):
        return own(k, far, 0) + own(k, near, 8)

    own_block_of_round_0()
    load(0)
    wait_local()
    fused(own_all(0))
    wait_more(0, 16)
    fused(passed(0))
    wait_more(1, 15 + 16)
    store_and_load(0, 1)
    wait_sent()
    fused(own_all(1))
    fused(passed(1))
    wait_more(2, 15)
    store_and_load(1, 2)
    wait_sent()
    fused(own_all(2))
    wait_more(0, 16)
    fused(passed(2))
    wait_more(3, 15)
    store_and_load(2, 3)
    fused(own_all(3))
    wait_more(2, 16)
    fused(passed(3))
    wait_more(1, 15)
    finish()
